import numpy as np, ml_dtypes
CORES = [51,54,179,182]
N = 4
BF = ml_dtypes.bfloat16
def f(rng, *shape):
    return (rng.standard_normal(shape, dtype=np.float32) * np.exp2(rng.integers(-2, 3, shape[:-1] + (1,)))).astype(BF)
def wide(rng, *shape):
    v = f(rng, *shape).astype(np.float32); k = shape[:-2] + (1, shape[-1])
    return (v * np.exp2(rng.integers(-6, 7, k)) * (rng.random(k) > 0.0625)).astype(BF)
def gentries(a):
    return np.ascontiguousarray(a.reshape(8, 16, -1).transpose(0, 2, 1)).reshape(8, -1)
def gtable(e):
    e = np.asarray(e); return np.ascontiguousarray(e.reshape(8, -1, 16).transpose(0, 2, 1)).reshape(128, -1).astype(np.int32)
L, K, R, D = 4096, 1024, 4, 2048
def corner(rng):
    return rng.integers(0, 4096 - D, (2, 1, 8, 1))
def walk(rng):
    v = np.repeat(rng.integers(-3, 4, (N, 8, L // 64)), 64, axis=2) + rng.integers(-1, 2, (N, 8, L))
    m = (rng.integers(0, D + 1, (N, 8, 1)) + np.add.accumulate(v, axis=2)) % (2 * D)
    return D - np.abs(m - D)
def listeners(rng, o):
    return rng.integers(D, L - 1, (N, 8, K)), o[0] + rng.integers(0, D + 1, (N, 8, K)), o[1] + rng.integers(0, D + 1, (N, 8, K))
def packed(X, Y, s, t, x, z):
    return {"track": (X * 4096 + Y).astype(np.int32), "sound": s, "when": np.stack([gtable(a) for a in t]), "place": np.stack([gtable(a) for a in x * 4096 + z])}
def setup_inputs(rng):
    o = corner(rng); t, x, z = listeners(rng, o)
    return packed(o[0] + walk(rng), o[1] + walk(rng), f(rng, N, 128, L), t, x, z)
def setup_inputs_ends(rng):
    o = np.zeros((2, 1, 8, 1), np.int64); o[:, :, 1::2] = 4095 - D
    X, Y = o[0] + walk(rng), o[1] + walk(rng); t, x, z = listeners(rng, o)
    for g in range(8):
        q = int(rng.integers(0, N)); c = int(o[0, 0, g, 0]); near, far = (c, c + D) if g % 2 == 0 else (c + D, c)
        X[q, g, :D + 1] = near; Y[q, g, :D + 1] = near
        t[:, g, 0] = D; x[:, g, 0] = far; z[:, g, 0] = far
        for r in range(N):
            p = (r + 1) % N; t[r, g, K - 1] = L - 2; x[r, g, K - 1] = X[p, g, L - 2]; z[r, g, K - 1] = Y[p, g, L - 2]
    return packed(X, Y, f(rng, N, 128, L), t, x, z)
def setup_inputs_jumps(rng):
    o = corner(rng); t, x, z = listeners(rng, o)
    return packed(o[0] + rng.integers(0, D + 1, (N, 8, L)), o[1] + rng.integers(0, D + 1, (N, 8, L)), f(rng, N, 128, L), t, x, z)
def setup_inputs_still(rng):
    o = corner(rng); t, x, z = listeners(rng, o); X, Y = o[0] + walk(rng), o[1] + walk(rng)
    q = int(rng.integers(0, N)); r = (q + 1) % N; w = (q + 2) % N
    X[q] = X[q, :, :1].copy(); Y[q] = Y[q, :, :1].copy()
    for a in (t, x, z): a[r, :4] = a[r, :4, :1].copy()
    t[w] = np.sort(t[w], axis=1); x[w] = x[w, :, :1].copy(); z[w] = z[w, :, :1].copy()
    return packed(X, Y, f(rng, N, 128, L), t, x, z)
def setup_inputs_sizes(rng):
    d = np.array([0, 4094, 3, 4000, 64, 3000, 500, 2049]).reshape(1, 8, 1)
    o = rng.integers(0, 4096 - d, (2, 1, 8, 1))
    h = lambda n: rng.integers(0, d + 1, (N, 8, n))
    t = rng.integers(d, L - 1, (N, 8, K)); t[:, 0, 0] = 0
    return packed(o[0] + h(L), o[1] + h(L), f(rng, N, 128, L), t, o[0] + h(K), o[1] + h(K))
def setup_inputs_spread(rng):
    d = setup_inputs(rng); d["sound"] = wide(rng, N, 128, L); return d
def check_inputs(d):
    bad = []; tr = np.asarray(d["track"]).astype(np.int64); pl = np.asarray(d["place"]).astype(np.int64); wh = np.asarray(d["when"]).astype(np.int64)
    if not np.isfinite(np.asarray(d["sound"]).astype(np.float32)).all(): bad.append("finite")
    if tr.min() < 0 or tr.max() >= 4096 * 4096: bad.append("track")
    if pl.min() < 0 or pl.max() >= 4096 * 4096: bad.append("place")
    if wh.min() < 0 or wh.max() > L - 2: bad.append("when")
    ok = True
    for r in range(N):
        t = gentries(wh[r]); w = gentries(pl[r])
        for q in range(N):
            e = np.clip(t, 0, L - 2)
            for i in range(R):
                v = np.take_along_axis(tr[q], e, 1)
                e = t - np.maximum(np.abs((v >> 12) - (w >> 12)), np.abs((v & 4095) - (w & 4095)))
                ok = ok and bool(e.min() >= 0) and bool(e.max() <= L - 2); e = np.clip(e, 0, L - 2)
    if not ok: bad.append("inside")
    return bad
def reference(track, sound, when, place):
    y = np.zeros((N, 128, K), np.float32); s = sound.astype(np.float32).reshape(N, 8, 16, L); tr = track.astype(np.int64)
    for r in range(N):
        t = gentries(when[r]).astype(np.int64); w = gentries(place[r]).astype(np.int64)
        for q in range(N):
            e = t
            for i in range(R):
                v = np.take_along_axis(tr[q], e, 1)
                e = t - np.maximum(np.abs((v >> 12) - (w >> 12)), np.abs((v & 4095) - (w & 4095)))
            u = np.take_along_axis(s[q], e[:, None, :], 2) + np.take_along_axis(s[q], e[:, None, :] + 1, 2)
            y[r] += u.astype(BF).astype(np.float32).reshape(128, K)
    return {"y": y}

@@ -1,0 +1,293 @@
+from concourse.bass import DstId, RemoteDMATransfer
+from concourse.mybir import AluOpType, ActivationFunctionType
+
+L, K = 4096, 1024
+C = K // 16
+HALF = 2048
+ROUNDS = 4
+NV = 68
+NS1 = 28
+
+SCRATCH = {
+    "wt": ("sbuf", [128, C], "int32"),
+    "pl": ("sbuf", [128, C], "int32"),
+    "xi": ("sbuf", [128, 2 * C], "int32"),
+    "tr": ("sbuf", [128, 256], "int32"),
+    "ti": ("sbuf", [128, 1024], "int32"),
+    "pc": ("sbuf", [128, 1024], "bfloat16"),
+    "win": ("sbuf", [128, L], "bfloat16"),
+    "ps": ("sbuf", [128, L], "bfloat16"),
+    "lsA": ("sbuf", [128, 6 * C], "float16"),
+    "lsB": ("sbuf", [128, 6 * C], "float16"),
+    "offA": ("sbuf", [128, 2 * C], "uint16"),
+    "offB": ("sbuf", [128, 2 * C], "uint16"),
+    "gA": ("sbuf", [128, 2 * K], "bfloat16"),
+    "gB": ("sbuf", [128, 2 * K], "bfloat16"),
+    "abA": ("sbuf", [128, 256], "float32"),
+    "abB": ("sbuf", [128, 256], "float32"),
+    "diag": ("sbuf", [128, 128], "int32"),
+    "sel": ("sbuf", [128, 16], "bfloat16"),
+    "i16": ("sbuf", [128, 384], "float16"),
+    "i32": ("sbuf", [128, 128], "float32"),
+    "ibf": ("sbuf", [128, 128], "bfloat16"),
+    "uo": ("sbuf", [128, 3 * K], "bfloat16"),
+    "ul": ("sbuf", [128, 4 * K], "bfloat16"),
+    "ys": ("sbuf", [128, K], "float32"),
+    "dA": ("psum", [128, 512], "float32"),
+    "dB": ("psum", [128, 512], "float32"),
+    "eA": ("psum", [128, 512], "float32"),
+    "eB": ("psum", [128, 512], "float32"),
+    "y0": ("psum", [128, 512], "float32"),
+    "y1": ("psum", [128, 512], "float32"),
+    "y2": ("psum", [128, 512], "float32"),
+    "y3": ("psum", [128, 512], "float32"),
+}
+SEMAPHORES = (["ldt", "ldp", "ldtr", "z1", "z2", "pv", "prep", "iot", "selc", "cst", "winr", "lsent", "la", "lb",
+               "sl0", "sl1", "acc", "us0", "us1", "usn", "uo0", "uo1", "ub0", "ub1", "un", "usent", "st"]
+              + ["ti%d" % k for k in range(4)] + ["pc%d" % k for k in range(4)]
+              + [s + c for s in ("gat", "ext", "abu", "abw", "dmm", "off") for c in "AB"]
+              + ["ym%d" % k for k in range(4)] + ["yv%d" % k for k in range(4)])
+
+
+def _bits(engs):
+    m = 0
+    for e in engs:
+        m |= 1 << e
+    return m
+
+
+def rank_program(g, core, T, topo):
+    rank = T.rank_of(core)
+    if rank is None:
+        return
+    cores = list(T.cores)
+    n = len(cores)
+    place_of = lambda c: (topo.host(c), topo.chip(c))
+    near_of = lambda r: [q for q in range(n) if q != r and place_of(cores[q]) == place_of(cores[r])]
+    far_of = lambda r: [q for q in range(n) if place_of(cores[q]) != place_of(cores[r])]
+    nb = near_of(rank)[0]
+    far = far_of(rank)
+    off_eng = topo.engines(core, cores[far[0]])
+    h = len(off_eng) // 2
+    far_mask = [_bits(off_eng[:h]), _bits(off_eng[h:])]
+    near_eng = [e for e in topo.engines(core, cores[nb]) if e not in off_eng]
+    near_mask = _bits(near_eng)
+    n_far, n_near = h, len(near_eng)
+    nb_rid, nb_pid = topo.addr(cores[nb], core)
+
+    def dst(q):
+        rid, pid = topo.addr(cores[q], core)
+        return DstId(rid=rid, pnc=pid)
+
+    S = T.sem
+    V, A, P, Y = g.vector, g.scalar, g.tensor, g.sync
+    add, mult = AluOpType.add, AluOpType.mult
+    shr, band = AluOpType.arith_shift_right, AluOpType.bitwise_and
+    COPY, ABS = ActivationFunctionType.Copy, ActivationFunctionType.Abs
+    W3 = 3 * C
+    slots = [(c, r) for r in range(ROUNDS) for c in "BA"]
+
+    Y.dma_start(T.wt[:], T.when[:]).then_inc(S.ldt, 16)
+    Y.dma_start(T.tr[:], T.track[:]).then_inc(S.ldtr, 16)
+    Y.wait_ge(S.z1, 1)
+    Y.wait_ge(S.z2, 2)
+    for k in (0, 2):
+        Y.wait_ge(S["pc%d" % k], 1)
+        Y.dma_start(T.win[k:128:16, :], T.pc[:, 256 * k:256 * k + 256]).then_inc(S.winr, 16)
+    Y.wait_ge(S.lsent, 2 * n_far + n_near)
+    Y.dma_start(T.ps[:, 0:HALF], T.sound[:, 0:HALF]).then_inc(S.sl0, 16)
+    Y.dma_start(T.ps[:, HALF:L], T.sound[:, HALF:L]).then_inc(S.sl1, 16)
+    for j in (0, 2):
+        Y.wait_ge(S["yv%d" % j], 1)
+        Y.dma_start(T.y[:, 256 * j:256 * j + 256], T.ys[:, 256 * j:256 * j + 256]).then_inc(S.st, 16)
+    Y.wait_ge(S.st, 64)
+
+    g.iota(T.diag[:], [[-1, 128]], 0, 1).then_inc(S.iot, 1)
+    g.iota(T.sel[:], [[0, 16]], 1, 0, allow_small_or_imprecise_dtypes=True).then_inc(S.selc, 1)
+    g.wait_ge(S.selc, 1)
+    g.affine_select(T.sel[:, 8:16], T.sel[:, 8:16], [[16, 8]], AluOpType.is_ge, -1.0, 1, -1).then_inc(S.selc, 1)
+    g.wait_ge(S.selc, 2)
+    g.affine_select(T.sel[:], T.sel[:], [[0, 2], [-16, 8]], AluOpType.is_ge, 0.0, 0, 1).then_inc(S.selc, 1)
+    g.wait_ge(S.selc, 3)
+    g.affine_select(T.sel[:], T.sel[:], [[0, 2], [16, 8]], AluOpType.is_ge, 0.0, 3, -1).then_inc(S.selc, 1)
+    g.wait_ge(S.prep, 3)
+    tr = []
+    for i, q in enumerate(far):
+        s = far_of(q).index(rank)
+        tr.append(RemoteDMATransfer(dst_ids=[dst(q)], dma_engine_mask=far_mask[i], remote_sem=S.lb,
+                                    src=T.lsA[:, 0:W3], dst=T.lsB[:, s * W3:(s + 1) * W3]))
+    g.remote_dma_fused(tr, local_sem=S.lsent)
+    g.remote_dma(T.lsA[:, W3:2 * W3], T.lsA[:, 0:W3], S.la, S.lsent, nb_pid, nb_rid, near_mask)
+    g.wait_ge(S.sl0, 16)
+    g.dma_start(T.ps[:, 0:HALF], T.sound[:, 1:HALF + 1], accum_op=add).then_inc(S.acc, 16)
+    g.wait_ge(S.sl1, 16)
+    g.dma_start(T.ps[:, HALF:L - 1], T.sound[:, HALF + 1:L], accum_op=add).then_inc(S.acc, 16)
+    for hh in range(2):
+        g.wait_ge(S["us%d" % hh], 2)
+        tr = []
+        for i, q in enumerate(far):
+            a = i * K + hh * 512
+            b = rank * K + hh * 512
+            tr.append(RemoteDMATransfer(dst_ids=[dst(q)], dma_engine_mask=far_mask[i], remote_sem=S["ub%d" % hh],
+                                        src=T.uo[:, a:a + 512], dst=T.ul[:, b:b + 512]))
+        g.remote_dma_fused(tr, local_sem=S.usent)
+    g.wait_ge(S.usn, 2)
+    g.remote_dma(T.ul[:, rank * K:(rank + 1) * K], T.uo[:, 2 * K:3 * K], S.un, S.usent, nb_pid, nb_rid, near_mask)
+    g.wait_ge(S.usent, 4 * n_far + n_near)
+
+    V.memset(T.win[:, 0:1536], 0.0).then_inc(S.z1, 1)
+    V.memset(T.win[:, 1536:2560], 0.0).then_inc(S.z2, 1)
+    V.wait_ge(S.ldp, 16)
+    V.tensor_scalar(T.xi[:, 0:C], T.pl[:], 12, None, shr).then_inc(S.pv, 1)
+    V.tensor_scalar(T.xi[:, C:2 * C], T.pl[:], 4095, None, band).then_inc(S.pv, 1)
+    V.wait_ge(S.ldt, 16)
+    V.tensor_scalar(T.lsA[:, 0:W3:3], T.wt[:], float(-HALF), None, add).then_inc(S.prep, 1)
+    V.wait_ge(S.pv, 2)
+    V.tensor_scalar(T.lsA[:, 1:W3:3], T.xi[:, 0:C], float(-HALF), None, add).then_inc(S.prep, 1)
+    V.tensor_scalar(T.lsA[:, 2:W3:3], T.xi[:, C:2 * C], float(-HALF), None, add).then_inc(S.prep, 1)
+    V.wait_ge(S.ldtr, 16)
+
+    def cut(k):
+        o = T.ti[:, 256 * k:256 * k + 256]
+        if k == 0:
+            ins = V.tensor_scalar(o, T.tr[:], 18, None, shr)
+        elif k == 3:
+            ins = V.tensor_scalar(o, T.tr[:], 63, None, band)
+        else:
+            ins = V.tensor_scalar(o, T.tr[:], 12 if k == 1 else 6, 63, shr, band)
+        ins.then_inc(S["ti%d" % k], 1)
+
+    def conv(k):
+        V.wait_ge(S["ti%d" % k], 1)
+        o, i = T.pc[:, 256 * k:256 * k + 256], T.ti[:, 256 * k:256 * k + 256]
+        if k % 2 == 0:
+            ins = V.tensor_scalar(o, i, -32.0, 64.0, add, mult)
+        else:
+            ins = V.tensor_copy(o, i)
+        ins.then_inc(S["pc%d" % k], 1)
+
+    cut(0); cut(1); conv(0); cut(2); conv(1); cut(3); conv(2); conv(3)
+    V.wait_ge(S.iot, 1)
+    eq = AluOpType.is_equal
+    V.tensor_scalar(T.i16[:, 0:128], T.diag[:], 0.0, -1.0, eq, mult).then_inc(S.cst, 1)
+    V.tensor_scalar(T.i16[:, 128:256], T.diag[:], 0.0, -1.0, eq, mult).then_inc(S.cst, 1)
+    V.tensor_scalar(T.i16[:, 256:384], T.diag[:], 0.0, 1.0, eq, mult).then_inc(S.cst, 1)
+    V.tensor_scalar(T.i32[:], T.diag[:], 0.0, -1.0, eq, mult).then_inc(S.cst, 1)
+    V.tensor_scalar(T.ibf[:], T.diag[:], 0.0, 1.0, eq, mult).then_inc(S.cst, 1)
+    V.wait_ge(S.lb, 2 * n_far)
+    V.tensor_scalar(T.offB[:], T.lsB[:, 0:2 * W3:3], float(HALF), None, add).then_inc(S.offB, 1)
+    V.wait_ge(S.winr, 64)
+    for s, (c, r) in enumerate(slots):
+        nv = C if s == 0 else NV
+        V.wait_ge(S["off" + c], r + 1)
+        V.tensor_copy(T["g" + c][:, 0:16 * nv], T.win[:, 0:L].indirect(T["off" + c][:, 0:nv])).then_inc(S["gat" + c], 1)
+        if s == 0:
+            V.wait_ge(S.la, n_near)
+            V.wait_ge(S.prep, 3)
+            V.tensor_scalar(T.offA[:], T.lsA[:, 0:2 * W3:3], float(HALF), None, add).then_inc(S.offA, 1)
+        else:
+            pc_, pr = slots[s - 1]
+            V.wait_ge(S["dmm" + pc_], pr + 1)
+            V.tensor_scalar(T["off" + pc_][:], T["e" + pc_][:, 0:128], float(HALF), None, add).then_inc(S["off" + pc_], 1)
+    V.wait_ge(S.acc, 32)
+    V.wait_ge(S.offB, ROUNDS + 1)
+    for hh in range(2):
+        V.tensor_copy(T.uo[:, 512 * hh:512 * hh + 512],
+                      T.ps[:, 0:L].indirect(T.offB[:, 32 * hh:32 * hh + 32])).then_inc(S["us%d" % hh], 1)
+    V.wait_ge(S.dmmA, ROUNDS)
+    V.tensor_scalar(T.offA[:], T.eA[:, 0:128], float(HALF), None, add).then_inc(S.offA, 1)
+    V.wait_ge(S.offA, ROUNDS + 1)
+    V.tensor_copy(T.uo[:, 2 * K:2 * K + 512], T.ps[:, 0:L].indirect(T.offA[:, C:C + 32])).then_inc(S.usn, 1)
+    V.tensor_copy(T.ul[:, rank * K:rank * K + 512], T.ps[:, 0:L].indirect(T.offA[:, 0:32])).then_inc(S.uo0, 1)
+
+    def wait_u(q_eng, seen, q, hh):
+        if q == rank:
+            key = ("uo%d" % hh, 1)
+        elif q == nb:
+            key = ("un", n_near)
+        else:
+            key = ("ub%d" % hh, 2 * n_far)
+        if key not in seen:
+            seen.append(key)
+            q_eng.wait_ge(S[key[0]], key[1])
+
+    seen = []
+    for j in range(4):
+        wait_u(V, seen, n - 1, j // 2)
+        V.wait_ge(S["ym%d" % j], 1)
+        b = (n - 1) * K + 256 * j
+        V.tensor_tensor(T.ys[:, 256 * j:256 * j + 256], T["y%d" % j][:, 0:256], T.ul[:, b:b + 256], add).then_inc(S["yv%d" % j], 1)
+
+    A.dma_start(T.pl[:], T.place[:]).then_inc(S.ldp, 16)
+    A.wait_ge(S.z1, 1)
+    A.activation(T.win[:, 2560:L], T.win[:, 0:1536], COPY).then_inc(S.z2, 1)
+    A.wait_ge(S.z2, 2)
+    for k in (1, 3):
+        A.wait_ge(S["pc%d" % k], 1)
+        A.dma_start(T.win[k:128:16, :], T.pc[:, 256 * k:256 * k + 256]).then_inc(S.winr, 16)
+    A.wait_ge(S.winr, 64)
+
+    def absolute(c, r):
+        A.wait_ge(S["ext" + c], r + 1)
+        A.activation(T["ab" + c][:, 0:128], T["d" + c][:, 0:128], ABS, scale=0.5).then_inc(S["abu" + c], 1)
+        A.activation(T["ab" + c][:, 128:256], T["d" + c][:, 128:256], ABS, scale=0.5).then_inc(S["abw" + c], 1)
+
+    def sgather(c, a, b):
+        A.activation(T["g" + c][:, 16 * a:16 * b], T.win[:, 0:L].indirect(T["off" + c][:, a:b]), COPY).then_inc(S["gat" + c], 1)
+
+    gat_count = {"A": [], "B": []}
+    tot = {"A": 0, "B": 0}
+    for s, (c, r) in enumerate(slots):
+        A.wait_ge(S["off" + c], r + 1)
+        if s == 0:
+            sgather(c, C, 2 * C)
+            tot[c] += 2
+        else:
+            sgather(c, NV, NV + NS1)
+            absolute(*slots[s - 1])
+            sgather(c, NV + NS1, 2 * C)
+            tot[c] += 3
+        gat_count[c].append(tot[c])
+    A.wait_ge(S.acc, 32)
+    A.wait_ge(S.offB, ROUNDS + 1)
+    A.activation(T.uo[:, K:K + 512], T.ps[:, 0:L].indirect(T.offB[:, C:C + 32]), COPY).then_inc(S.us0, 1)
+    absolute("A", ROUNDS - 1)
+    A.activation(T.uo[:, K + 512:2 * K], T.ps[:, 0:L].indirect(T.offB[:, C + 32:2 * C]), COPY).then_inc(S.us1, 1)
+    A.wait_ge(S.offA, ROUNDS + 1)
+    A.activation(T.uo[:, 2 * K + 512:3 * K], T.ps[:, 0:L].indirect(T.offA[:, C + 32:2 * C]), COPY).then_inc(S.usn, 1)
+    A.activation(T.ul[:, rank * K + 512:(rank + 1) * K], T.ps[:, 0:L].indirect(T.offA[:, 32:C]), COPY).then_inc(S.uo1, 1)
+    for j in (1, 3):
+        A.wait_ge(S["yv%d" % j], 1)
+        A.dma_start(T.y[:, 256 * j:256 * j + 256], T.ys[:, 256 * j:256 * j + 256]).then_inc(S.st, 16)
+
+    def init(c):
+        ls, d = T["ls" + c], T["d" + c]
+        P.matmul(d[:, 0:256], ls[:, 1:2 * W3:3], T.i16[:, 0:256], True, False)
+        P.matmul(d[:, 0:256], ls[:, 2:2 * W3:3], T.i16[:, 128:384], False, False)
+
+    P.wait_ge(S.cst, 5)
+    P.wait_ge(S.selc, 4)
+    P.wait_ge(S.lb, 2 * n_far)
+    init("B")
+    for s, (c, r) in enumerate(slots):
+        P.wait_ge(S["gat" + c], gat_count[c][r])
+        for i in range(16):
+            ins = P.matmul(T["d" + c][:, i:256:16], T["g" + c][:, i:2 * K:16], T.sel[:], False, i == 15)
+        ins.then_inc(S["ext" + c], 1)
+        P.matmul(T["e" + c][:, 0:128], T.i16[:, 256:384], T["ls" + c][:, 0:2 * W3:3], True, False)
+        if s + 1 < len(slots):
+            if s == 0:
+                P.wait_ge(S.la, n_near)
+                P.wait_ge(S.prep, 3)
+            init(slots[s + 1][0])
+        P.wait_ge(S["abu" + c], r + 1)
+        P.matmul(T["e" + c][:, 0:128], T["ab" + c][:, 0:128], T.i32[:], False, False)
+        P.wait_ge(S["abw" + c], r + 1)
+        P.matmul(T["e" + c][:, 0:128], T["ab" + c][:, 128:256], T.i32[:], False, True).then_inc(S["dmm" + c], 1)
+    seen = []
+    for j in range(4):
+        for q in range(n - 1):
+            wait_u(P, seen, q, j // 2)
+            b = q * K + 256 * j
+            ins = P.matmul(T["y%d" % j][:, 0:256], T.ibf[:], T.ul[:, b:b + 256], q == 0, q == n - 2)
+        ins.then_inc(S["ym%d" % j], 1)

@@ -1,12 +1,16 @@
 from concourse.bass import DstId, RemoteDMATransfer
 from concourse.mybir import AluOpType, ActivationFunctionType
 
-L, K = 4096, 1024
+L, K, NR = 4096, 1024, 4
 C = K // 16
 HALF = 2048
-ROUNDS = 4
 NV = 68
 NS1 = 28
+NVU = 36
+NP = 4
+PW = L // NP
+NPASS = 9
+BLOCKS = (12, 12, 8)
 
 SCRATCH = {
     "wt": ("sbuf", [128, C], "int32"),
@@ -16,37 +20,37 @@ SCRATCH = {
     "ti": ("sbuf", [128, 1024], "int32"),
     "pc": ("sbuf", [128, 1024], "bfloat16"),
     "win": ("sbuf", [128, L], "bfloat16"),
-    "ps": ("sbuf", [128, L], "bfloat16"),
     "lsA": ("sbuf", [128, 6 * C], "float16"),
     "lsB": ("sbuf", [128, 6 * C], "float16"),
     "offA": ("sbuf", [128, 2 * C], "uint16"),
     "offB": ("sbuf", [128, 2 * C], "uint16"),
+    "eN": ("sbuf", [128, C], "uint16"),
+    "eF": ("sbuf", [128, 2 * C], "uint16"),
     "gA": ("sbuf", [128, 2 * K], "bfloat16"),
     "gB": ("sbuf", [128, 2 * K], "bfloat16"),
     "abA": ("sbuf", [128, 256], "float32"),
     "abB": ("sbuf", [128, 256], "float32"),
+    "abC": ("sbuf", [128, 256], "float32"),
     "diag": ("sbuf", [128, 128], "int32"),
     "sel": ("sbuf", [128, 16], "bfloat16"),
     "i16": ("sbuf", [128, 384], "float16"),
     "i32": ("sbuf", [128, 128], "float32"),
     "ibf": ("sbuf", [128, 128], "bfloat16"),
-    "uo": ("sbuf", [128, 3 * K], "bfloat16"),
-    "ul": ("sbuf", [128, 4 * K], "bfloat16"),
+    "ul": ("sbuf", [128, NR * K], "bfloat16"),
     "ys": ("sbuf", [128, K], "float32"),
-    "dA": ("psum", [128, 512], "float32"),
-    "dB": ("psum", [128, 512], "float32"),
-    "eA": ("psum", [128, 512], "float32"),
-    "eB": ("psum", [128, 512], "float32"),
-    "y0": ("psum", [128, 512], "float32"),
-    "y1": ("psum", [128, 512], "float32"),
-    "y2": ("psum", [128, 512], "float32"),
-    "y3": ("psum", [128, 512], "float32"),
 }
+for _q in range(NR):
+    SCRATCH["ps%d" % _q] = ("sbuf", [128, L], "bfloat16")
+for _b in ("dA", "dB", "dC", "eA", "eB", "eC", "y0", "y1"):
+    SCRATCH[_b] = ("psum", [128, 512], "float32")
+
 SEMAPHORES = (["ldt", "ldp", "ldtr", "z1", "z2", "pv", "prep", "iot", "selc", "cst", "winr", "lsent", "la", "lb",
-               "sl0", "sl1", "acc", "us0", "us1", "usn", "uo0", "uo1", "ub0", "ub1", "un", "usent", "st"]
+               "oown", "onear", "ofar", "psent", "pn", "pf0", "pf1", "hsent", "en", "ef0", "ef1", "esent",
+               "uo", "un", "ua", "st"]
               + ["ti%d" % k for k in range(4)] + ["pc%d" % k for k in range(4)]
-              + [s + c for s in ("gat", "ext", "abu", "abw", "dmm", "off") for c in "AB"]
-              + ["ym%d" % k for k in range(4)] + ["yv%d" % k for k in range(4)])
+              + [s + "%d" % k for s in ("sl", "acc", "hp") for k in range(NP)]
+              + [s + "%d" % p for s in ("gat", "ext", "abu", "abw", "dmm", "off") for p in range(NPASS)]
+              + [s + "%d" % k for s in ("ub", "ym", "yv") for k in range(2 * len(BLOCKS))])
 
 
 def _bits(engs):
@@ -57,50 +61,85 @@ def _bits(engs):
 
 
 def rank_program(g, core, T, topo):
-    rank = T.rank_of(core)
-    if rank is None:
-        return
     cores = list(T.cores)
     n = len(cores)
+    S = T.sem
     place_of = lambda c: (topo.host(c), topo.chip(c))
-    near_of = lambda r: [q for q in range(n) if q != r and place_of(cores[q]) == place_of(cores[r])]
-    far_of = lambda r: [q for q in range(n) if place_of(cores[q]) != place_of(cores[r])]
-    nb = near_of(rank)[0]
+    near_of = lambda r: [q for q in range(n) if q != r and place_of(cores[q]) == place_of(cores[r])][0]
+    far_of = lambda r: sorted((q for q in range(n) if place_of(cores[q]) != place_of(cores[r])),
+                              key=lambda q: topo.die(cores[q]) != topo.die(cores[r]))
+    helper_of = lambda q: [c for c in topo.cores_of(cores[far_of(q)[0]])
+                           if c not in cores and topo.die(c) == topo.die(cores[q])][0]
+
+    def dst(c):
+        rid, pid = topo.addr(c, core)
+        return DstId(rid=rid, pnc=pid)
+
+    def piece(q, k):
+        return T["ps%d" % q][:, PW * k:PW * (k + 1)]
+
+    rank = T.rank_of(core)
+    if rank is None:
+        for q in range(n):
+            if helper_of(q) == core:
+                engs = topo.engines(core, cores[far_of(q)[0]])
+                nin = len(topo.engines(cores[q], core))
+                for k in range(NP):
+                    g.wait_ge(S["hp%d" % k], nin)
+                    g.remote_dma_fused([RemoteDMATransfer(dst_ids=[dst(cores[r])], dma_engine_mask=_bits(engs[i::2]),
+                                                          remote_sem=S["pf%d" % i], src=piece(q, k), dst=piece(q, k))
+                                        for i, r in enumerate(far_of(q))], local_sem=S.hsent)
+                g.wait_ge(S.hsent, NP * len(engs))
+        return
+
+    nb = near_of(rank)
     far = far_of(rank)
     off_eng = topo.engines(core, cores[far[0]])
     h = len(off_eng) // 2
-    far_mask = [_bits(off_eng[:h]), _bits(off_eng[h:])]
+    n_off = len(off_eng)
     near_eng = [e for e in topo.engines(core, cores[nb]) if e not in off_eng]
-    near_mask = _bits(near_eng)
-    n_far, n_near = h, len(near_eng)
+    near_mask, off_mask = _bits(near_eng), _bits(off_eng)
+    n_near = len(near_eng)
+    n_fan = len(topo.engines(helper_of(far[0]), core)) // 2
     nb_rid, nb_pid = topo.addr(cores[nb], core)
 
-    def dst(q):
-        rid, pid = topo.addr(cores[q], core)
-        return DstId(rid=rid, pnc=pid)
-
-    S = T.sem
     V, A, P, Y = g.vector, g.scalar, g.tensor, g.sync
     add, mult = AluOpType.add, AluOpType.mult
     shr, band = AluOpType.arith_shift_right, AluOpType.bitwise_and
     COPY, ABS = ActivationFunctionType.Copy, ActivationFunctionType.Abs
     W3 = 3 * C
-    slots = [(c, r) for r in range(ROUNDS) for c in "BA"]
+    ps = lambda q: T["ps%d" % q][:, 0:L]
+    passes = [("AB"[p % 2], 0, 2 * C, "AB"[p % 2]) for p in range(7)] + [("B", 0, C, "B"), ("B", C, 2 * C, "C")]
+    banks = ("dA", "eA", "dB", "eB", "y0", "y1")
+    blocks = []
+    for j, w in enumerate(BLOCKS):
+        for e in range(2):
+            blocks.append((e * C // 2 + sum(BLOCKS[:j]), w, banks[2 * j + e]))
+    nblk = len(blocks)
+
+    def load_sound(k):
+        Y.dma_start(piece(rank, k), T.sound[:, PW * k:PW * (k + 1)]).then_inc(S["sl%d" % k], 16)
 
     Y.dma_start(T.wt[:], T.when[:]).then_inc(S.ldt, 16)
     Y.dma_start(T.tr[:], T.track[:]).then_inc(S.ldtr, 16)
+    for k in range(NP // 2):
+        load_sound(k)
     Y.wait_ge(S.z1, 1)
     Y.wait_ge(S.z2, 2)
-    for k in (0, 2):
+    for k in (1, 3):
         Y.wait_ge(S["pc%d" % k], 1)
         Y.dma_start(T.win[k:128:16, :], T.pc[:, 256 * k:256 * k + 256]).then_inc(S.winr, 16)
-    Y.wait_ge(S.lsent, 2 * n_far + n_near)
-    Y.dma_start(T.ps[:, 0:HALF], T.sound[:, 0:HALF]).then_inc(S.sl0, 16)
-    Y.dma_start(T.ps[:, HALF:L], T.sound[:, HALF:L]).then_inc(S.sl1, 16)
-    for j in (0, 2):
-        Y.wait_ge(S["yv%d" % j], 1)
-        Y.dma_start(T.y[:, 256 * j:256 * j + 256], T.ys[:, 256 * j:256 * j + 256]).then_inc(S.st, 16)
-    Y.wait_ge(S.st, 64)
+    for k in range(NP // 2, NP):
+        load_sound(k)
+
+    def store(q_eng, j):
+        a, w, _ = blocks[j]
+        q_eng.wait_ge(S["yv%d" % j], 1)
+        q_eng.dma_start(T.y[:, 16 * a:16 * (a + w)], T.ys[:, 16 * a:16 * (a + w)]).then_inc(S.st, 16)
+
+    for j in range(nblk - 1):
+        store(Y, j)
+    Y.wait_ge(S.st, 16 * nblk)
 
     g.iota(T.diag[:], [[-1, 128]], 0, 1).then_inc(S.iot, 1)
     g.iota(T.sel[:], [[0, 16]], 1, 0, allow_small_or_imprecise_dtypes=True).then_inc(S.selc, 1)
@@ -111,29 +150,67 @@ def rank_program(g, core, T, topo):
     g.wait_ge(S.selc, 3)
     g.affine_select(T.sel[:], T.sel[:], [[0, 2], [16, 8]], AluOpType.is_ge, 0.0, 3, -1).then_inc(S.selc, 1)
     g.wait_ge(S.prep, 3)
-    tr = []
-    for i, q in enumerate(far):
-        s = far_of(q).index(rank)
-        tr.append(RemoteDMATransfer(dst_ids=[dst(q)], dma_engine_mask=far_mask[i], remote_sem=S.lb,
-                                    src=T.lsA[:, 0:W3], dst=T.lsB[:, s * W3:(s + 1) * W3]))
-    g.remote_dma_fused(tr, local_sem=S.lsent)
     g.remote_dma(T.lsA[:, W3:2 * W3], T.lsA[:, 0:W3], S.la, S.lsent, nb_pid, nb_rid, near_mask)
-    g.wait_ge(S.sl0, 16)
-    g.dma_start(T.ps[:, 0:HALF], T.sound[:, 1:HALF + 1], accum_op=add).then_inc(S.acc, 16)
-    g.wait_ge(S.sl1, 16)
-    g.dma_start(T.ps[:, HALF:L - 1], T.sound[:, HALF + 1:L], accum_op=add).then_inc(S.acc, 16)
-    for hh in range(2):
-        g.wait_ge(S["us%d" % hh], 2)
-        tr = []
-        for i, q in enumerate(far):
-            a = i * K + hh * 512
-            b = rank * K + hh * 512
-            tr.append(RemoteDMATransfer(dst_ids=[dst(q)], dma_engine_mask=far_mask[i], remote_sem=S["ub%d" % hh],
-                                        src=T.uo[:, a:a + 512], dst=T.ul[:, b:b + 512]))
-        g.remote_dma_fused(tr, local_sem=S.usent)
-    g.wait_ge(S.usn, 2)
-    g.remote_dma(T.ul[:, rank * K:(rank + 1) * K], T.uo[:, 2 * K:3 * K], S.un, S.usent, nb_pid, nb_rid, near_mask)
-    g.wait_ge(S.usent, 4 * n_far + n_near)
+    g.remote_dma_fused([RemoteDMATransfer(dst_ids=[dst(cores[q])], dma_engine_mask=_bits(off_eng[i * h:(i + 1) * h]),
+                                          remote_sem=S.lb, src=T.lsA[:, 0:W3], dst=T.lsB[:, i * W3:(i + 1) * W3])
+                        for i, q in enumerate(far)], local_sem=S.lsent)
+
+    def pair_sum(k):
+        a, b = PW * k, min(PW * (k + 1), L - 1)
+        g.wait_ge(S["sl%d" % k], 16)
+        g.dma_start(T["ps%d" % rank][:, a:b], T.sound[:, a + 1:b + 1], accum_op=add).then_inc(S["acc%d" % k], 16)
+
+    def send_piece(k):
+        g.wait_ge(S["acc%d" % k], 16)
+        g.remote_dma_fused([RemoteDMATransfer(dst_ids=[dst(helper_of(rank))], dma_engine_mask=off_mask,
+                                              remote_sem=S["hp%d" % k], src=piece(rank, k), dst=piece(rank, k)),
+                            RemoteDMATransfer(dst_ids=[dst(cores[nb])], dma_engine_mask=near_mask,
+                                              remote_sem=S.pn, src=piece(rank, k), dst=piece(rank, k))], local_sem=S.psent)
+
+    g.wait_ge(S.pc3, 1)
+    pair_sum(0)
+    for k in range(NP):
+        if k + 1 < NP:
+            pair_sum(k + 1)
+        send_piece(k)
+    g.wait_ge(S.off6, 1)
+    g.remote_dma(T.eN[:], T.offA[:, C:2 * C], S.en, S.esent, nb_pid, nb_rid, near_mask)
+    for i, q in enumerate(far):
+        rid, pid = topo.addr(cores[q], core)
+        g.wait_ge(S["off%d" % (7 + i)], 1)
+        g.remote_dma(T.eF[:, i * C:(i + 1) * C], T.offB[:, i * C:(i + 1) * C], S["ef%d" % i], S.esent, pid, rid, off_mask)
+    g.wait_ge(S.lsent, n_off + n_near)
+    g.wait_ge(S.psent, NP * (n_off + n_near))
+    g.wait_ge(S.esent, 2 * n_off + n_near)
+
+    ngat = [0] * NPASS
+
+    def gather(E, out, win, off):
+        if E is V:
+            return V.tensor_copy(out, win.indirect(off))
+        return A.activation(out, win.indirect(off), COPY)
+
+    def track_gather(E, p, a, b):
+        c = passes[p][0]
+        gather(E, T["g" + c][:, 16 * a:16 * b], T.win[:, 0:L], T["off" + c][:, a:b]).then_inc(S["gat%d" % p], 1)
+        ngat[p] += 1
+
+    def sound_gather(E, q, off, o, a, b, sem):
+        gather(E, T.ul[:, q * K + 16 * a:q * K + 16 * b], ps(q), off[:, o + a:o + b]).then_inc(sem, 1)
+
+    def wait_off(E, p):
+        if p >= 2:
+            E.wait_ge(S["off%d" % min(p - 2, 5)], 1)
+        elif p == 1:
+            E.wait_ge(S.ofar, 1)
+
+    def own_sums(E):
+        for k in range(NP):
+            E.wait_ge(S["acc%d" % k], 16)
+
+    def far_in(E, i):
+        E.wait_ge(S["pf%d" % i], NP * n_fan)
+        E.wait_ge(S["ef%d" % i], n_off)
 
     V.memset(T.win[:, 0:1536], 0.0).then_inc(S.z1, 1)
     V.memset(T.win[:, 1536:2560], 0.0).then_inc(S.z2, 1)
@@ -167,6 +244,7 @@ def rank_program(g, core, T, topo):
         ins.then_inc(S["pc%d" % k], 1)
 
     cut(0); cut(1); conv(0); cut(2); conv(1); cut(3); conv(2); conv(3)
+    V.tensor_copy(T.offA[:, 0:C], T.wt[:]).then_inc(S.oown, 1)
     V.wait_ge(S.iot, 1)
     eq = AluOpType.is_equal
     V.tensor_scalar(T.i16[:, 0:128], T.diag[:], 0.0, -1.0, eq, mult).then_inc(S.cst, 1)
@@ -174,120 +252,172 @@ def rank_program(g, core, T, topo):
     V.tensor_scalar(T.i16[:, 256:384], T.diag[:], 0.0, 1.0, eq, mult).then_inc(S.cst, 1)
     V.tensor_scalar(T.i32[:], T.diag[:], 0.0, -1.0, eq, mult).then_inc(S.cst, 1)
     V.tensor_scalar(T.ibf[:], T.diag[:], 0.0, 1.0, eq, mult).then_inc(S.cst, 1)
-    V.wait_ge(S.lb, 2 * n_far)
-    V.tensor_scalar(T.offB[:], T.lsB[:, 0:2 * W3:3], float(HALF), None, add).then_inc(S.offB, 1)
-    V.wait_ge(S.winr, 64)
-    for s, (c, r) in enumerate(slots):
-        nv = C if s == 0 else NV
-        V.wait_ge(S["off" + c], r + 1)
-        V.tensor_copy(T["g" + c][:, 0:16 * nv], T.win[:, 0:L].indirect(T["off" + c][:, 0:nv])).then_inc(S["gat" + c], 1)
-        if s == 0:
-            V.wait_ge(S.la, n_near)
-            V.wait_ge(S.prep, 3)
-            V.tensor_scalar(T.offA[:], T.lsA[:, 0:2 * W3:3], float(HALF), None, add).then_inc(S.offA, 1)
-        else:
-            pc_, pr = slots[s - 1]
-            V.wait_ge(S["dmm" + pc_], pr + 1)
-            V.tensor_scalar(T["off" + pc_][:], T["e" + pc_][:, 0:128], float(HALF), None, add).then_inc(S["off" + pc_], 1)
-    V.wait_ge(S.acc, 32)
-    V.wait_ge(S.offB, ROUNDS + 1)
-    for hh in range(2):
-        V.tensor_copy(T.uo[:, 512 * hh:512 * hh + 512],
-                      T.ps[:, 0:L].indirect(T.offB[:, 32 * hh:32 * hh + 32])).then_inc(S["us%d" % hh], 1)
-    V.wait_ge(S.dmmA, ROUNDS)
-    V.tensor_scalar(T.offA[:], T.eA[:, 0:128], float(HALF), None, add).then_inc(S.offA, 1)
-    V.wait_ge(S.offA, ROUNDS + 1)
-    V.tensor_copy(T.uo[:, 2 * K:2 * K + 512], T.ps[:, 0:L].indirect(T.offA[:, C:C + 32])).then_inc(S.usn, 1)
-    V.tensor_copy(T.ul[:, rank * K:rank * K + 512], T.ps[:, 0:L].indirect(T.offA[:, 0:32])).then_inc(S.uo0, 1)
 
-    def wait_u(q_eng, seen, q, hh):
-        if q == rank:
-            key = ("uo%d" % hh, 1)
-        elif q == nb:
-            key = ("un", n_near)
-        else:
-            key = ("ub%d" % hh, 2 * n_far)
+    def offsets(p):
+        c, a, b, z = passes[p]
+        V.wait_ge(S["dmm%d" % p], 1)
+        V.tensor_scalar(T["off" + c][:, a:b], T["e" + z][:, 0:b - a], float(HALF), None, add).then_inc(S["off%d" % p], 1)
+
+    V.wait_ge(S.winr, 64)
+    V.wait_ge(S.oown, 1)
+    track_gather(V, 0, 0, 30)
+    V.wait_ge(S.la, n_near)
+    V.tensor_scalar(T.offA[:, C:2 * C], T.lsA[:, W3:2 * W3:3], float(HALF), None, add).then_inc(S.onear, 1)
+    V.wait_ge(S.onear, 1)
+    track_gather(V, 0, C, C + 30)
+    V.wait_ge(S.lb, n_off)
+    V.tensor_scalar(T.offB[:], T.lsB[:, 0:2 * W3:3], float(HALF), None, add).then_inc(S.ofar, 1)
+    for p in range(1, 7):
+        wait_off(V, p)
+        track_gather(V, p, 0, NV)
+        offsets(p - 1)
+    wait_off(V, 7)
+    track_gather(V, 7, 0, NVU)
+    track_gather(V, 8, C, C + NVU)
+    offsets(6)
+    own_sums(V)
+    V.wait_ge(S.off6, 1)
+    sound_gather(V, rank, T.offA, 0, 0, 24, S.uo)
+    offsets(7)
+    sound_gather(V, rank, T.offA, 0, 24, 40, S.uo)
+    offsets(8)
+    V.wait_ge(S.pn, NP * n_near)
+    V.wait_ge(S.en, n_near)
+    sound_gather(V, nb, T.eN, 0, 0, C // 2, S.un)
+    far_in(V, 0)
+    sound_gather(V, far[0], T.eF, 0, 0, C // 2, S.ua)
+    far_in(V, 1)
+
+    def late_gather(E, j):
+        a, w, _ = blocks[j]
+        sound_gather(E, far[1], T.eF, C, a, a + w, S["ub%d" % j])
+
+    def u_ready(E, q, j, seen):
+        key = ("uo", 4) if q == rank else ("un", 2) if q == nb else ("ua", 2) if q == far[0] else ("ub%d" % j, 1)
         if key not in seen:
             seen.append(key)
-            q_eng.wait_ge(S[key[0]], key[1])
+            E.wait_ge(S[key[0]], key[1])
 
-    seen = []
-    for j in range(4):
-        wait_u(V, seen, n - 1, j // 2)
+    seen_v = []
+
+    def out_v(j):
+        a, w, z = blocks[j]
+        u_ready(V, n - 1, j, seen_v)
         V.wait_ge(S["ym%d" % j], 1)
-        b = (n - 1) * K + 256 * j
-        V.tensor_tensor(T.ys[:, 256 * j:256 * j + 256], T["y%d" % j][:, 0:256], T.ul[:, b:b + 256], add).then_inc(S["yv%d" % j], 1)
+        b = (n - 1) * K + 16 * a
+        V.tensor_tensor(T.ys[:, 16 * a:16 * (a + w)], T[z][:, 0:16 * w], T.ul[:, b:b + 16 * w], add).then_inc(S["yv%d" % j], 1)
+
+    def out_s(j):
+        a, w, z = blocks[j]
+        A.wait_ge(S["ym%d" % j], 1)
+        A.activation(T.ys[:, 16 * a:16 * (a + w)], T[z][:, 0:16 * w], COPY).then_inc(S["yv%d" % j], 1)
+
+    def last_stage(E, e, out):
+        js = list(range(e, nblk, 2))
+        late_gather(E, js[0])
+        for i, j in enumerate(js):
+            if i + 1 < len(js):
+                late_gather(E, js[i + 1])
+            out(j)
+
+    last_stage(V, 0, out_v)
 
     A.dma_start(T.pl[:], T.place[:]).then_inc(S.ldp, 16)
     A.wait_ge(S.z1, 1)
     A.activation(T.win[:, 2560:L], T.win[:, 0:1536], COPY).then_inc(S.z2, 1)
     A.wait_ge(S.z2, 2)
-    for k in (1, 3):
+    for k in (0, 2):
         A.wait_ge(S["pc%d" % k], 1)
         A.dma_start(T.win[k:128:16, :], T.pc[:, 256 * k:256 * k + 256]).then_inc(S.winr, 16)
+
+    def absolute(p):
+        c, a, b, z = passes[p]
+        m = b - a
+        A.wait_ge(S["ext%d" % p], 1)
+        A.activation(T["ab" + z][0:m, 0:128], T["d" + z][0:m, 0:128], ABS, scale=0.5).then_inc(S["abu%d" % p], 1)
+        A.activation(T["ab" + z][0:m, 128:256], T["d" + z][0:m, 128:256], ABS, scale=0.5).then_inc(S["abw%d" % p], 1)
+
     A.wait_ge(S.winr, 64)
+    A.wait_ge(S.oown, 1)
+    track_gather(A, 0, 30, C)
+    A.wait_ge(S.onear, 1)
+    track_gather(A, 0, C + 30, 2 * C)
+    for p in range(1, 7):
+        wait_off(A, p)
+        track_gather(A, p, NV, NV + NS1)
+        absolute(p - 1)
+        track_gather(A, p, NV + NS1, 2 * C)
+    wait_off(A, 7)
+    track_gather(A, 7, NVU, C)
+    absolute(6)
+    track_gather(A, 8, C + NVU, 2 * C)
+    absolute(7)
+    own_sums(A)
+    A.wait_ge(S.off6, 1)
+    sound_gather(A, rank, T.offA, 0, 40, 52, S.uo)
+    absolute(8)
+    sound_gather(A, rank, T.offA, 0, 52, C, S.uo)
+    A.wait_ge(S.pn, NP * n_near)
+    A.wait_ge(S.en, n_near)
+    sound_gather(A, nb, T.eN, 0, C // 2, C, S.un)
+    far_in(A, 0)
+    sound_gather(A, far[0], T.eF, 0, C // 2, C, S.ua)
+    far_in(A, 1)
+    last_stage(A, 1, out_s)
+    store(A, nblk - 1)
 
-    def absolute(c, r):
-        A.wait_ge(S["ext" + c], r + 1)
-        A.activation(T["ab" + c][:, 0:128], T["d" + c][:, 0:128], ABS, scale=0.5).then_inc(S["abu" + c], 1)
-        A.activation(T["ab" + c][:, 128:256], T["d" + c][:, 128:256], ABS, scale=0.5).then_inc(S["abw" + c], 1)
+    def init(p):
+        c, a, b, z = passes[p]
+        ls, d = T["ls" + c], T["d" + z][0:b - a, 0:256]
+        P.matmul(d, ls[:, 3 * a + 1:3 * b:3], T.i16[:, 0:256], True, False)
+        P.matmul(d, ls[:, 3 * a + 2:3 * b:3], T.i16[:, 128:384], False, False)
 
-    def sgather(c, a, b):
-        A.activation(T["g" + c][:, 16 * a:16 * b], T.win[:, 0:L].indirect(T["off" + c][:, a:b]), COPY).then_inc(S["gat" + c], 1)
+    def times(p):
+        c, a, b, z = passes[p]
+        P.matmul(T["e" + z][:, 0:b - a], T.i16[:, 256:384], T["ls" + c][:, 3 * a:3 * b:3], True, False)
 
-    gat_count = {"A": [], "B": []}
-    tot = {"A": 0, "B": 0}
-    for s, (c, r) in enumerate(slots):
-        A.wait_ge(S["off" + c], r + 1)
-        if s == 0:
-            sgather(c, C, 2 * C)
-            tot[c] += 2
-        else:
-            sgather(c, NV, NV + NS1)
-            absolute(*slots[s - 1])
-            sgather(c, NV + NS1, 2 * C)
-            tot[c] += 3
-        gat_count[c].append(tot[c])
-    A.wait_ge(S.acc, 32)
-    A.wait_ge(S.offB, ROUNDS + 1)
-    A.activation(T.uo[:, K:K + 512], T.ps[:, 0:L].indirect(T.offB[:, C:C + 32]), COPY).then_inc(S.us0, 1)
-    absolute("A", ROUNDS - 1)
-    A.activation(T.uo[:, K + 512:2 * K], T.ps[:, 0:L].indirect(T.offB[:, C + 32:2 * C]), COPY).then_inc(S.us1, 1)
-    A.wait_ge(S.offA, ROUNDS + 1)
-    A.activation(T.uo[:, 2 * K + 512:3 * K], T.ps[:, 0:L].indirect(T.offA[:, C + 32:2 * C]), COPY).then_inc(S.usn, 1)
-    A.activation(T.ul[:, rank * K + 512:(rank + 1) * K], T.ps[:, 0:L].indirect(T.offA[:, 32:C]), COPY).then_inc(S.uo1, 1)
-    for j in (1, 3):
-        A.wait_ge(S["yv%d" % j], 1)
-        A.dma_start(T.y[:, 256 * j:256 * j + 256], T.ys[:, 256 * j:256 * j + 256]).then_inc(S.st, 16)
+    def turn(p):
+        c, a, b, z = passes[p]
+        P.wait_ge(S["gat%d" % p], ngat[p])
+        for i in range(16):
+            ins = P.matmul(T["d" + z][0:b - a, i:256:16], T["g" + c][:, 16 * a + i:16 * b:16], T.sel[:], False, i == 15)
+        ins.then_inc(S["ext%d" % p], 1)
 
-    def init(c):
-        ls, d = T["ls" + c], T["d" + c]
-        P.matmul(d[:, 0:256], ls[:, 1:2 * W3:3], T.i16[:, 0:256], True, False)
-        P.matmul(d[:, 0:256], ls[:, 2:2 * W3:3], T.i16[:, 128:384], False, False)
+    def back(p):
+        c, a, b, z = passes[p]
+        m = b - a
+        P.wait_ge(S["abu%d" % p], 1)
+        P.matmul(T["e" + z][:, 0:m], T["ab" + z][0:m, 0:128], T.i32[0:m, 0:m], False, False)
+        P.wait_ge(S["abw%d" % p], 1)
+        P.matmul(T["e" + z][:, 0:m], T["ab" + z][0:m, 128:256], T.i32[0:m, 0:m], False, True).then_inc(S["dmm%d" % p], 1)
 
     P.wait_ge(S.cst, 5)
     P.wait_ge(S.selc, 4)
-    P.wait_ge(S.lb, 2 * n_far)
-    init("B")
-    for s, (c, r) in enumerate(slots):
-        P.wait_ge(S["gat" + c], gat_count[c][r])
-        for i in range(16):
-            ins = P.matmul(T["d" + c][:, i:256:16], T["g" + c][:, i:2 * K:16], T.sel[:], False, i == 15)
-        ins.then_inc(S["ext" + c], 1)
-        P.matmul(T["e" + c][:, 0:128], T.i16[:, 256:384], T["ls" + c][:, 0:2 * W3:3], True, False)
-        if s + 1 < len(slots):
-            if s == 0:
-                P.wait_ge(S.la, n_near)
-                P.wait_ge(S.prep, 3)
-            init(slots[s + 1][0])
-        P.wait_ge(S["abu" + c], r + 1)
-        P.matmul(T["e" + c][:, 0:128], T["ab" + c][:, 0:128], T.i32[:], False, False)
-        P.wait_ge(S["abw" + c], r + 1)
-        P.matmul(T["e" + c][:, 0:128], T["ab" + c][:, 128:256], T.i32[:], False, True).then_inc(S["dmm" + c], 1)
-    seen = []
-    for j in range(4):
-        for q in range(n - 1):
-            wait_u(P, seen, q, j // 2)
-            b = q * K + 256 * j
-            ins = P.matmul(T["y%d" % j][:, 0:256], T.ibf[:], T.ul[:, b:b + 256], q == 0, q == n - 2)
+    P.wait_ge(S.prep, 3)
+    P.wait_ge(S.la, n_near)
+    init(0)
+    for p in range(7):
+        turn(p)
+        times(p)
+        if p == 0:
+            P.wait_ge(S.lb, n_off)
+        init(p + 1)
+        back(p)
+        if p == 5:
+            init(8)
+            times(8)
+    turn(7)
+    times(7)
+    turn(8)
+    back(7)
+    back(8)
+    P.wait_ge(S.off6, 1)
+    P.wait_ge(S.off7, 1)
+    seen_p = []
+    for j, (a, w, z) in enumerate(blocks):
+        last = n - 1 if j % 2 == 0 else n
+        for q in range(last):
+            u_ready(P, q, j, seen_p)
+            b = q * K + 16 * a
+            ins = P.matmul(T[z][:, 0:16 * w], T.ibf[:], T.ul[:, b:b + 16 * w], q == 0, q == last - 1)
         ins.then_inc(S["ym%d" % j], 1)

from concourse.bass import DstId, RemoteDMATransfer
from concourse.mybir import AluOpType, ActivationFunctionType

L, K, NR = 4096, 1024, 4
C = K // 16
HALF = 2048
NV = 68
NS1 = 28
NVU = 36
NP = 4
PW = L // NP
NPASS = 9
BLOCKS = (12, 12, 8)

SCRATCH = {
    "wt": ("sbuf", [128, C], "int32"),
    "pl": ("sbuf", [128, C], "int32"),
    "xi": ("sbuf", [128, 2 * C], "int32"),
    "tr": ("sbuf", [128, 256], "int32"),
    "ti": ("sbuf", [128, 1024], "int32"),
    "pc": ("sbuf", [128, 1024], "bfloat16"),
    "win": ("sbuf", [128, L], "bfloat16"),
    "lsA": ("sbuf", [128, 6 * C], "float16"),
    "lsB": ("sbuf", [128, 6 * C], "float16"),
    "offA": ("sbuf", [128, 2 * C], "uint16"),
    "offB": ("sbuf", [128, 2 * C], "uint16"),
    "eN": ("sbuf", [128, C], "uint16"),
    "eF": ("sbuf", [128, 2 * C], "uint16"),
    "gA": ("sbuf", [128, 2 * K], "bfloat16"),
    "gB": ("sbuf", [128, 2 * K], "bfloat16"),
    "abA": ("sbuf", [128, 256], "float32"),
    "abB": ("sbuf", [128, 256], "float32"),
    "abC": ("sbuf", [128, 256], "float32"),
    "diag": ("sbuf", [128, 128], "int32"),
    "sel": ("sbuf", [128, 16], "bfloat16"),
    "i16": ("sbuf", [128, 384], "float16"),
    "i32": ("sbuf", [128, 128], "float32"),
    "ibf": ("sbuf", [128, 128], "bfloat16"),
    "ul": ("sbuf", [128, NR * K], "bfloat16"),
    "ys": ("sbuf", [128, K], "float32"),
}
for _q in range(NR):
    SCRATCH["ps%d" % _q] = ("sbuf", [128, L], "bfloat16")
for _b in ("dA", "dB", "dC", "eA", "eB", "eC", "y0", "y1"):
    SCRATCH[_b] = ("psum", [128, 512], "float32")

SEMAPHORES = (["ldt", "ldp", "ldtr", "z1", "z2", "pv", "prep", "iot", "selc", "cst", "winr", "lsent", "la", "lb",
               "oown", "onear", "ofar", "psent", "pn", "pf0", "pf1", "hsent", "en", "ef0", "ef1", "esent",
               "uo", "un", "ua", "st"]
              + ["ti%d" % k for k in range(4)] + ["pc%d" % k for k in range(4)]
              + [s + "%d" % k for s in ("sl", "acc", "hp") for k in range(NP)]
              + [s + "%d" % p for s in ("gat", "ext", "abu", "abw", "dmm", "off") for p in range(NPASS)]
              + [s + "%d" % k for s in ("ub", "ym", "yv") for k in range(2 * len(BLOCKS))])


def _bits(engs):
    m = 0
    for e in engs:
        m |= 1 << e
    return m


def rank_program(g, core, T, topo):
    cores = list(T.cores)
    n = len(cores)
    S = T.sem
    place_of = lambda c: (topo.host(c), topo.chip(c))
    near_of = lambda r: [q for q in range(n) if q != r and place_of(cores[q]) == place_of(cores[r])][0]
    far_of = lambda r: sorted((q for q in range(n) if place_of(cores[q]) != place_of(cores[r])),
                              key=lambda q: topo.die(cores[q]) != topo.die(cores[r]))
    helper_of = lambda q: [c for c in topo.cores_of(cores[far_of(q)[0]])
                           if c not in cores and topo.die(c) == topo.die(cores[q])][0]

    def dst(c):
        rid, pid = topo.addr(c, core)
        return DstId(rid=rid, pnc=pid)

    def piece(q, k):
        return T["ps%d" % q][:, PW * k:PW * (k + 1)]

    rank = T.rank_of(core)
    if rank is None:
        for q in range(n):
            if helper_of(q) == core:
                engs = topo.engines(core, cores[far_of(q)[0]])
                nin = len(topo.engines(cores[q], core))
                for k in range(NP):
                    g.wait_ge(S["hp%d" % k], nin)
                    g.remote_dma_fused([RemoteDMATransfer(dst_ids=[dst(cores[r])], dma_engine_mask=_bits(engs[i::2]),
                                                          remote_sem=S["pf%d" % i], src=piece(q, k), dst=piece(q, k))
                                        for i, r in enumerate(far_of(q))], local_sem=S.hsent)
                g.wait_ge(S.hsent, NP * len(engs))
        return

    nb = near_of(rank)
    far = far_of(rank)
    off_eng = topo.engines(core, cores[far[0]])
    h = len(off_eng) // 2
    n_off = len(off_eng)
    near_eng = [e for e in topo.engines(core, cores[nb]) if e not in off_eng]
    near_mask, off_mask = _bits(near_eng), _bits(off_eng)
    n_near = len(near_eng)
    n_fan = len(topo.engines(helper_of(far[0]), core)) // 2
    nb_rid, nb_pid = topo.addr(cores[nb], core)

    V, A, P, Y = g.vector, g.scalar, g.tensor, g.sync
    add, mult = AluOpType.add, AluOpType.mult
    shr, band = AluOpType.arith_shift_right, AluOpType.bitwise_and
    COPY, ABS = ActivationFunctionType.Copy, ActivationFunctionType.Abs
    W3 = 3 * C
    ps = lambda q: T["ps%d" % q][:, 0:L]
    passes = [("AB"[p % 2], 0, 2 * C, "AB"[p % 2]) for p in range(7)] + [("B", 0, C, "B"), ("B", C, 2 * C, "C")]
    banks = ("dA", "eA", "dB", "eB", "y0", "y1")
    blocks = []
    for j, w in enumerate(BLOCKS):
        for e in range(2):
            blocks.append((e * C // 2 + sum(BLOCKS[:j]), w, banks[2 * j + e]))
    nblk = len(blocks)

    def load_sound(k):
        Y.dma_start(piece(rank, k), T.sound[:, PW * k:PW * (k + 1)]).then_inc(S["sl%d" % k], 16)

    Y.dma_start(T.wt[:], T.when[:]).then_inc(S.ldt, 16)
    Y.dma_start(T.tr[:], T.track[:]).then_inc(S.ldtr, 16)
    for k in range(NP // 2):
        load_sound(k)
    Y.wait_ge(S.z1, 1)
    Y.wait_ge(S.z2, 2)
    for k in (1, 3):
        Y.wait_ge(S["pc%d" % k], 1)
        Y.dma_start(T.win[k:128:16, :], T.pc[:, 256 * k:256 * k + 256]).then_inc(S.winr, 16)
    for k in range(NP // 2, NP):
        load_sound(k)

    def store(q_eng, j):
        a, w, _ = blocks[j]
        q_eng.wait_ge(S["yv%d" % j], 1)
        q_eng.dma_start(T.y[:, 16 * a:16 * (a + w)], T.ys[:, 16 * a:16 * (a + w)]).then_inc(S.st, 16)

    for j in range(nblk - 1):
        store(Y, j)
    Y.wait_ge(S.st, 16 * nblk)

    g.iota(T.diag[:], [[-1, 128]], 0, 1).then_inc(S.iot, 1)
    g.iota(T.sel[:], [[0, 16]], 1, 0, allow_small_or_imprecise_dtypes=True).then_inc(S.selc, 1)
    g.wait_ge(S.selc, 1)
    g.affine_select(T.sel[:, 8:16], T.sel[:, 8:16], [[16, 8]], AluOpType.is_ge, -1.0, 1, -1).then_inc(S.selc, 1)
    g.wait_ge(S.selc, 2)
    g.affine_select(T.sel[:], T.sel[:], [[0, 2], [-16, 8]], AluOpType.is_ge, 0.0, 0, 1).then_inc(S.selc, 1)
    g.wait_ge(S.selc, 3)
    g.affine_select(T.sel[:], T.sel[:], [[0, 2], [16, 8]], AluOpType.is_ge, 0.0, 3, -1).then_inc(S.selc, 1)
    g.wait_ge(S.prep, 3)
    g.remote_dma(T.lsA[:, W3:2 * W3], T.lsA[:, 0:W3], S.la, S.lsent, nb_pid, nb_rid, near_mask)
    g.remote_dma_fused([RemoteDMATransfer(dst_ids=[dst(cores[q])], dma_engine_mask=_bits(off_eng[i * h:(i + 1) * h]),
                                          remote_sem=S.lb, src=T.lsA[:, 0:W3], dst=T.lsB[:, i * W3:(i + 1) * W3])
                        for i, q in enumerate(far)], local_sem=S.lsent)

    def pair_sum(k):
        a, b = PW * k, min(PW * (k + 1), L - 1)
        g.wait_ge(S["sl%d" % k], 16)
        g.dma_start(T["ps%d" % rank][:, a:b], T.sound[:, a + 1:b + 1], accum_op=add).then_inc(S["acc%d" % k], 16)

    def send_piece(k):
        g.wait_ge(S["acc%d" % k], 16)
        g.remote_dma_fused([RemoteDMATransfer(dst_ids=[dst(helper_of(rank))], dma_engine_mask=off_mask,
                                              remote_sem=S["hp%d" % k], src=piece(rank, k), dst=piece(rank, k)),
                            RemoteDMATransfer(dst_ids=[dst(cores[nb])], dma_engine_mask=near_mask,
                                              remote_sem=S.pn, src=piece(rank, k), dst=piece(rank, k))], local_sem=S.psent)

    g.wait_ge(S.pc3, 1)
    pair_sum(0)
    for k in range(NP):
        if k + 1 < NP:
            pair_sum(k + 1)
        send_piece(k)
    g.wait_ge(S.off6, 1)
    g.remote_dma(T.eN[:], T.offA[:, C:2 * C], S.en, S.esent, nb_pid, nb_rid, near_mask)
    for i, q in enumerate(far):
        rid, pid = topo.addr(cores[q], core)
        g.wait_ge(S["off%d" % (7 + i)], 1)
        g.remote_dma(T.eF[:, i * C:(i + 1) * C], T.offB[:, i * C:(i + 1) * C], S["ef%d" % i], S.esent, pid, rid, off_mask)
    g.wait_ge(S.lsent, n_off + n_near)
    g.wait_ge(S.psent, NP * (n_off + n_near))
    g.wait_ge(S.esent, 2 * n_off + n_near)

    ngat = [0] * NPASS

    def gather(E, out, win, off):
        if E is V:
            return V.tensor_copy(out, win.indirect(off))
        return A.activation(out, win.indirect(off), COPY)

    def track_gather(E, p, a, b):
        c = passes[p][0]
        gather(E, T["g" + c][:, 16 * a:16 * b], T.win[:, 0:L], T["off" + c][:, a:b]).then_inc(S["gat%d" % p], 1)
        ngat[p] += 1

    def sound_gather(E, q, off, o, a, b, sem):
        gather(E, T.ul[:, q * K + 16 * a:q * K + 16 * b], ps(q), off[:, o + a:o + b]).then_inc(sem, 1)

    def wait_off(E, p):
        if p >= 2:
            E.wait_ge(S["off%d" % min(p - 2, 5)], 1)
        elif p == 1:
            E.wait_ge(S.ofar, 1)

    def own_sums(E):
        for k in range(NP):
            E.wait_ge(S["acc%d" % k], 16)

    def far_in(E, i):
        E.wait_ge(S["pf%d" % i], NP * n_fan)
        E.wait_ge(S["ef%d" % i], n_off)

    V.memset(T.win[:, 0:1536], 0.0).then_inc(S.z1, 1)
    V.memset(T.win[:, 1536:2560], 0.0).then_inc(S.z2, 1)
    V.wait_ge(S.ldp, 16)
    V.tensor_scalar(T.xi[:, 0:C], T.pl[:], 12, None, shr).then_inc(S.pv, 1)
    V.tensor_scalar(T.xi[:, C:2 * C], T.pl[:], 4095, None, band).then_inc(S.pv, 1)
    V.wait_ge(S.ldt, 16)
    V.tensor_scalar(T.lsA[:, 0:W3:3], T.wt[:], float(-HALF), None, add).then_inc(S.prep, 1)
    V.wait_ge(S.pv, 2)
    V.tensor_scalar(T.lsA[:, 1:W3:3], T.xi[:, 0:C], float(-HALF), None, add).then_inc(S.prep, 1)
    V.tensor_scalar(T.lsA[:, 2:W3:3], T.xi[:, C:2 * C], float(-HALF), None, add).then_inc(S.prep, 1)
    V.wait_ge(S.ldtr, 16)

    def cut(k):
        o = T.ti[:, 256 * k:256 * k + 256]
        if k == 0:
            ins = V.tensor_scalar(o, T.tr[:], 18, None, shr)
        elif k == 3:
            ins = V.tensor_scalar(o, T.tr[:], 63, None, band)
        else:
            ins = V.tensor_scalar(o, T.tr[:], 12 if k == 1 else 6, 63, shr, band)
        ins.then_inc(S["ti%d" % k], 1)

    def conv(k):
        V.wait_ge(S["ti%d" % k], 1)
        o, i = T.pc[:, 256 * k:256 * k + 256], T.ti[:, 256 * k:256 * k + 256]
        if k % 2 == 0:
            ins = V.tensor_scalar(o, i, -32.0, 64.0, add, mult)
        else:
            ins = V.tensor_copy(o, i)
        ins.then_inc(S["pc%d" % k], 1)

    cut(0); cut(1); conv(0); cut(2); conv(1); cut(3); conv(2); conv(3)
    V.tensor_copy(T.offA[:, 0:C], T.wt[:]).then_inc(S.oown, 1)
    V.wait_ge(S.iot, 1)
    eq = AluOpType.is_equal
    V.tensor_scalar(T.i16[:, 0:128], T.diag[:], 0.0, -1.0, eq, mult).then_inc(S.cst, 1)
    V.tensor_scalar(T.i16[:, 128:256], T.diag[:], 0.0, -1.0, eq, mult).then_inc(S.cst, 1)
    V.tensor_scalar(T.i16[:, 256:384], T.diag[:], 0.0, 1.0, eq, mult).then_inc(S.cst, 1)
    V.tensor_scalar(T.i32[:], T.diag[:], 0.0, -1.0, eq, mult).then_inc(S.cst, 1)
    V.tensor_scalar(T.ibf[:], T.diag[:], 0.0, 1.0, eq, mult).then_inc(S.cst, 1)

    def offsets(p):
        c, a, b, z = passes[p]
        V.wait_ge(S["dmm%d" % p], 1)
        V.tensor_scalar(T["off" + c][:, a:b], T["e" + z][:, 0:b - a], float(HALF), None, add).then_inc(S["off%d" % p], 1)

    V.wait_ge(S.winr, 64)
    V.wait_ge(S.oown, 1)
    track_gather(V, 0, 0, 30)
    V.wait_ge(S.la, n_near)
    V.tensor_scalar(T.offA[:, C:2 * C], T.lsA[:, W3:2 * W3:3], float(HALF), None, add).then_inc(S.onear, 1)
    V.wait_ge(S.onear, 1)
    track_gather(V, 0, C, C + 30)
    V.wait_ge(S.lb, n_off)
    V.tensor_scalar(T.offB[:], T.lsB[:, 0:2 * W3:3], float(HALF), None, add).then_inc(S.ofar, 1)
    for p in range(1, 7):
        wait_off(V, p)
        track_gather(V, p, 0, NV)
        offsets(p - 1)
    wait_off(V, 7)
    track_gather(V, 7, 0, NVU)
    track_gather(V, 8, C, C + NVU)
    offsets(6)
    own_sums(V)
    V.wait_ge(S.off6, 1)
    sound_gather(V, rank, T.offA, 0, 0, 24, S.uo)
    offsets(7)
    sound_gather(V, rank, T.offA, 0, 24, 40, S.uo)
    offsets(8)
    V.wait_ge(S.pn, NP * n_near)
    V.wait_ge(S.en, n_near)
    sound_gather(V, nb, T.eN, 0, 0, C // 2, S.un)
    far_in(V, 0)
    sound_gather(V, far[0], T.eF, 0, 0, C // 2, S.ua)
    far_in(V, 1)

    def late_gather(E, j):
        a, w, _ = blocks[j]
        sound_gather(E, far[1], T.eF, C, a, a + w, S["ub%d" % j])

    def u_ready(E, q, j, seen):
        key = ("uo", 4) if q == rank else ("un", 2) if q == nb else ("ua", 2) if q == far[0] else ("ub%d" % j, 1)
        if key not in seen:
            seen.append(key)
            E.wait_ge(S[key[0]], key[1])

    seen_v = []

    def out_v(j):
        a, w, z = blocks[j]
        u_ready(V, n - 1, j, seen_v)
        V.wait_ge(S["ym%d" % j], 1)
        b = (n - 1) * K + 16 * a
        V.tensor_tensor(T.ys[:, 16 * a:16 * (a + w)], T[z][:, 0:16 * w], T.ul[:, b:b + 16 * w], add).then_inc(S["yv%d" % j], 1)

    def out_s(j):
        a, w, z = blocks[j]
        A.wait_ge(S["ym%d" % j], 1)
        A.activation(T.ys[:, 16 * a:16 * (a + w)], T[z][:, 0:16 * w], COPY).then_inc(S["yv%d" % j], 1)

    def last_stage(E, e, out):
        js = list(range(e, nblk, 2))
        late_gather(E, js[0])
        for i, j in enumerate(js):
            if i + 1 < len(js):
                late_gather(E, js[i + 1])
            out(j)

    last_stage(V, 0, out_v)

    A.dma_start(T.pl[:], T.place[:]).then_inc(S.ldp, 16)
    A.wait_ge(S.z1, 1)
    A.activation(T.win[:, 2560:L], T.win[:, 0:1536], COPY).then_inc(S.z2, 1)
    A.wait_ge(S.z2, 2)
    for k in (0, 2):
        A.wait_ge(S["pc%d" % k], 1)
        A.dma_start(T.win[k:128:16, :], T.pc[:, 256 * k:256 * k + 256]).then_inc(S.winr, 16)

    def absolute(p):
        c, a, b, z = passes[p]
        m = b - a
        A.wait_ge(S["ext%d" % p], 1)
        A.activation(T["ab" + z][0:m, 0:128], T["d" + z][0:m, 0:128], ABS, scale=0.5).then_inc(S["abu%d" % p], 1)
        A.activation(T["ab" + z][0:m, 128:256], T["d" + z][0:m, 128:256], ABS, scale=0.5).then_inc(S["abw%d" % p], 1)

    A.wait_ge(S.winr, 64)
    A.wait_ge(S.oown, 1)
    track_gather(A, 0, 30, C)
    A.wait_ge(S.onear, 1)
    track_gather(A, 0, C + 30, 2 * C)
    for p in range(1, 7):
        wait_off(A, p)
        track_gather(A, p, NV, NV + NS1)
        absolute(p - 1)
        track_gather(A, p, NV + NS1, 2 * C)
    wait_off(A, 7)
    track_gather(A, 7, NVU, C)
    absolute(6)
    track_gather(A, 8, C + NVU, 2 * C)
    absolute(7)
    own_sums(A)
    A.wait_ge(S.off6, 1)
    sound_gather(A, rank, T.offA, 0, 40, 52, S.uo)
    absolute(8)
    sound_gather(A, rank, T.offA, 0, 52, C, S.uo)
    A.wait_ge(S.pn, NP * n_near)
    A.wait_ge(S.en, n_near)
    sound_gather(A, nb, T.eN, 0, C // 2, C, S.un)
    far_in(A, 0)
    sound_gather(A, far[0], T.eF, 0, C // 2, C, S.ua)
    far_in(A, 1)
    last_stage(A, 1, out_s)
    store(A, nblk - 1)

    def init(p):
        c, a, b, z = passes[p]
        ls, d = T["ls" + c], T["d" + z][0:b - a, 0:256]
        P.matmul(d, ls[:, 3 * a + 1:3 * b:3], T.i16[:, 0:256], True, False)
        P.matmul(d, ls[:, 3 * a + 2:3 * b:3], T.i16[:, 128:384], False, False)

    def times(p):
        c, a, b, z = passes[p]
        P.matmul(T["e" + z][:, 0:b - a], T.i16[:, 256:384], T["ls" + c][:, 3 * a:3 * b:3], True, False)

    def turn(p):
        c, a, b, z = passes[p]
        P.wait_ge(S["gat%d" % p], ngat[p])
        for i in range(16):
            ins = P.matmul(T["d" + z][0:b - a, i:256:16], T["g" + c][:, 16 * a + i:16 * b:16], T.sel[:], False, i == 15)
        ins.then_inc(S["ext%d" % p], 1)

    def back(p):
        c, a, b, z = passes[p]
        m = b - a
        P.wait_ge(S["abu%d" % p], 1)
        P.matmul(T["e" + z][:, 0:m], T["ab" + z][0:m, 0:128], T.i32[0:m, 0:m], False, False)
        P.wait_ge(S["abw%d" % p], 1)
        P.matmul(T["e" + z][:, 0:m], T["ab" + z][0:m, 128:256], T.i32[0:m, 0:m], False, True).then_inc(S["dmm%d" % p], 1)

    P.wait_ge(S.cst, 5)
    P.wait_ge(S.selc, 4)
    P.wait_ge(S.prep, 3)
    P.wait_ge(S.la, n_near)
    init(0)
    for p in range(7):
        turn(p)
        times(p)
        if p == 0:
            P.wait_ge(S.lb, n_off)
        init(p + 1)
        back(p)
        if p == 5:
            init(8)
            times(8)
    turn(7)
    times(7)
    turn(8)
    back(7)
    back(8)
    P.wait_ge(S.off6, 1)
    P.wait_ge(S.off7, 1)
    seen_p = []
    for j, (a, w, z) in enumerate(blocks):
        last = n - 1 if j % 2 == 0 else n
        for q in range(last):
            u_ready(P, q, j, seen_p)
            b = q * K + 16 * a
            ins = P.matmul(T[z][:, 0:16 * w], T.ibf[:], T.ul[:, b:b + 16 * w], q == 0, q == last - 1)
        ins.then_inc(S["ym%d" % j], 1)
